import numpy as np
import ml_dtypes


def mxq(x, axis, fmt="e4m3"):
    dtype, down = {"e4m3": (ml_dtypes.float8_e4m3fn, 7), "e5m2": (ml_dtypes.float8_e5m2, 14)}[fmt]
    v = np.moveaxis(np.asarray(x, np.float32).astype(ml_dtypes.bfloat16).astype(np.float64), axis, -1)
    blocks = v.reshape(v.shape[:-1] + (-1, 32))
    amax = np.abs(blocks).max(-1, keepdims=True)
    byte = np.maximum(np.where(amax > 0, np.frexp(amax)[1] - 1 + 127, 0) - down, 1)
    scale = np.exp2(byte - 127.0)
    codes = (blocks / scale).astype(np.float32).astype(dtype).astype(np.float64)
    return np.moveaxis((codes * scale).reshape(v.shape), -1, axis)


WIDE = False


def mx_kscale(k):
    if not WIDE:
        return np.ones(k)
    levels = np.array([10, -10, 5, -5, 0])
    if k % 512:
        return np.exp2(np.random.permutation(np.resize(levels, k // 32))).repeat(32)
    a = np.empty((k // 512, 16))
    for p in range(k // 512):
        a[p, :8] = np.random.permutation(np.resize(levels, 8))
        for g in range(8):
            far = levels[np.abs(levels - a[p, g]) >= 10]
            a[p, g + 8] = far[np.random.randint(len(far))]
    return np.exp2(a.ravel()).repeat(32)


def f64(x):
    return np.asarray(x).astype(np.float64)


def striped(idx):
    return np.tile(idx.reshape(-1, 16).T, (8, 1)).astype(np.uint16)


def unstriped(offs):
    return offs[:16].T.reshape(-1).astype(np.int64)


def striped8(idx):
    return np.concatenate([x.reshape(-1, 16).T for x in idx]).astype(np.uint16)


def runs(offs, k):
    lists = np.stack([offs[16 * r : 16 * r + 16].T.reshape(-1) for r in range(8)]).astype(np.int64)
    return lists[np.arange(k) % 512 // 64]


def pack_weight(w):
    k, n = w.shape
    w = f64(np.asarray(w, np.float32).astype(ml_dtypes.bfloat16)).reshape(k // 32, 32, n)
    amax = np.abs(w).max(1)
    byte = np.clip(np.where(amax > 0, np.frexp(amax)[1] - 1 + 127 - 7, 1), 1, 254)
    scaled = (w * np.exp2(127.0 - byte)[:, None, :]).reshape(k, n).astype(np.float32)
    words = np.ascontiguousarray(scaled.reshape(k // 512, 128, 4, n).transpose(0, 1, 3, 2)).astype(ml_dtypes.float8_e4m3fn).view(np.uint8)
    return words, np.ascontiguousarray(byte.astype(np.uint8).reshape(k // 512, 16, n))


def unpack_weight(words, scales):
    g, p, n, _ = words.shape
    vals = np.ascontiguousarray(words).view(ml_dtypes.float8_e4m3fn).astype(np.float64) * np.repeat(np.exp2(scales.astype(np.float64) - 127.0), 8, axis=1)[..., None]
    return vals.transpose(0, 1, 3, 2).reshape(g * 512, n)


E2M1 = np.array([0.0, 0.5, 1.0, 1.5, 2.0, 3.0, 4.0, 6.0, -0.0, -0.5, -1.0, -1.5, -2.0, -3.0, -4.0, -6.0])


def pack_fp4(w):
    k, n = w.shape
    w = f64(np.asarray(w, np.float32).astype(ml_dtypes.bfloat16)).reshape(k // 32, 32, n)
    amax = np.abs(w).max(1)
    mant, ex = np.frexp(amax / 6.0)
    byte = np.clip(np.where(amax > 0, np.where(mant > 0.5, ex, ex - 1) + 127, 1), 1, 254)
    scaled = (w * np.exp2(127.0 - byte)[:, None, :]).reshape(k, n).astype(np.float32)
    c = np.ascontiguousarray(scaled.reshape(k // 512, 128, 4, n).transpose(0, 1, 3, 2)).astype(ml_dtypes.float4_e2m1fn).view(np.uint8) & 0xF
    words = (c[..., 0::2] | (c[..., 1::2] << 4)).reshape(k // 512, 128, 2 * n)
    return np.ascontiguousarray(words), np.ascontiguousarray(byte.astype(np.uint8).reshape(k // 512, 16, n))


def unpack_fp4(words, scales):
    g, _, n = scales.shape
    words = np.ascontiguousarray(words).reshape(g, 128, n, 2)
    nib = np.empty((g, 128, n, 4), np.uint8)
    nib[..., 0::2] = words & 0xF
    nib[..., 1::2] = words >> 4
    vals = E2M1[nib] * np.repeat(np.exp2(scales.astype(np.float64) - 127.0), 8, axis=1)[..., None]
    return vals.transpose(0, 1, 3, 2).reshape(g * 512, n)


def relu(v):
    return np.maximum(v, 0.0)

def planes(y):
    n, m = y.shape
    v = y.astype(np.float32).astype(ml_dtypes.bfloat16).astype(np.float64).reshape(n // 32, 32, m)
    top = np.abs(v).max(1)
    byte = np.clip(np.where(top > 0, np.frexp(top)[1] - 1 + 127 - 7, 1), 1, 254)
    codes = (v * np.exp2(127.0 - byte)[:, None, :]).reshape(n, m).astype(np.float32).astype(ml_dtypes.float8_e4m3fn).view(np.uint8)
    words = codes.reshape(n // 512, 128, 4, m).transpose(0, 1, 3, 2)
    return np.ascontiguousarray(words), np.ascontiguousarray(byte.astype(np.uint8).reshape(n // 512, 16, m))


K, T, S, N, H, U = 512, 2048, 512, 512, 512, 512


def setup_inputs():
    n = np.random.standard_normal
    s = mx_kscale(K)[:, None]
    u = mx_kscale(H)
    packed_xT = pack_weight(n((K, T)) * s)
    packed_w1 = pack_fp4(n((K, H)) / np.sqrt(K) / s)
    packed_w2 = pack_fp4(n((H, N)) / np.sqrt(H) / u[:, None])
    return {
        "x_words": packed_xT[0],
        "x_scales": packed_xT[1],
        "w1_words": packed_w1[0],
        "w1_scales": packed_w1[1],
        "cf1": (n((H, U)) * u[:, None]).astype(np.float32),
        "cf2": (n((H, U)) * u[:, None]).astype(np.float32),
        "cf3": (n((H, U)) * u[:, None]).astype(np.float32),
        "w2_words": packed_w2[0],
        "w2_scales": packed_w2[1],
        "offs": striped(np.random.permutation(T)[:S]),
        "fn": striped8(np.random.randint(0, U, (8, S))),
    }


def reference(x_words, x_scales, w1_words, w1_scales, cf1, cf2, cf3, w2_words, w2_scales, offs, fn):
    xq = unpack_weight(x_words, x_scales)[:, unstriped(offs)]
    y = unpack_fp4(w1_words, w1_scales).T @ xq
    z = relu(y + 0.75) * (f64(cf1)[np.arange(H)[:, None], runs(fn, H)]) + relu(y) * (f64(cf2)[np.arange(H)[:, None], runs(fn, H)]) + relu(y + -0.75) * (f64(cf3)[np.arange(H)[:, None], runs(fn, H)])
    out_0 = unpack_fp4(w2_words, w2_scales).T @ mxq(z, 0, "e4m3")
    return (out_0,) + planes(out_0)

@@ -1,0 +1,224 @@
+from contextlib import ExitStack
+
+import concourse.mybir as mybir
+from concourse.masks import make_identity
+
+F32 = mybir.dt.float32
+BF16 = mybir.dt.bfloat16
+I32 = mybir.dt.int32
+U32 = mybir.dt.uint32
+U16 = mybir.dt.uint16
+U8 = mybir.dt.uint8
+FP8X4 = mybir.dt.float8_e4m3fn_x4
+FP4X4 = mybir.dt.float4_e2m1fn_x4
+RELU = mybir.ActivationFunctionType.Relu
+MULT = mybir.AluOpType.mult
+
+P = 128
+T = 2048
+S = 512
+D = 512
+FLOPS = 2 * 2 * D * D * S
+BIASES = (0.75, 0.0, -0.75)
+PICK = 256
+CHUNKS = (256, 128, 128)
+
+
+def tile_picked_kan8_none_po_kernel(tc, x_words, x_scales, w1_words, w1_scales, cf1, cf2, cf3, w2_words, w2_scales, offs, fn, out_0, out_1, out_2):
+    nc = tc.nc
+    with ExitStack() as ctx:
+        sb = ctx.enter_context(tc.tile_pool(name="sb", bufs=1))
+        ps = ctx.enter_context(tc.psum_pool(name="ps", bufs=8))
+
+        def tile(name, shape, dtype, tag=""):
+            return sb.tile(shape, dtype, name=name, tag=tag or name, align_bytes=64)
+
+        def bank(name, shape):
+            return ps.tile(shape, F32, name=name, tag="bank")
+
+        def load_scales(queues, plane, scales):
+            for q, queue in enumerate(queues):
+                queue.dma_start(out=plane[32 * q : 32 * q + 4, :].bitcast(I32), in_=scales[0, 4 * q : 4 * q + 4, :].bitcast(I32))
+
+        offs_sb = tile("offs_sb", [P, S // 16], U16)
+        fn_sb = tile("fn_sb", [P, S // 16], U16)
+        xw = tile("xw", [P, T], I32)
+        xs = tile("xs", [P, T], U8)
+        s1_raw = tile("s1_raw", [P, D], U8)
+        w_sb = [tile("w_sb%d" % i, [P, 2 * D], U8) for i in range(2)]
+        s_sb = [tile("s_sb%d" % i, [P, D], U8) for i in range(2)]
+        ident = tile("ident", [P, P], F32)
+        warm = tile("warm", [P, 1], F32)
+
+        def deal_words(i, raw):
+            nc.vector.tensor_copy(
+                out=w_sb[i][:].rearrange("p (t m b) -> p t m b", t=4, b=2),
+                in_=raw[:].rearrange("p (m t b) -> p t m b", t=4, b=2),
+            )
+
+        nc.vector.memset(xs[:].bitcast(I32), 0)
+        nc.gpsimd.memset(s1_raw[:].bitcast(I32), 0)
+
+        with tc.tile_pool(name="head", bufs=1) as head:
+            w1_raw = head.tile([P, 2 * D], U8, name="w1_raw", align_bytes=64)
+            w2_raw = tile("w2_raw", [P, 2 * D], U8)
+            nc.sync.dma_start(offs_sb[:], offs)
+            nc.sync.dma_start(out=w1_raw[:].bitcast(I32), in_=w1_words[0].bitcast(I32))
+            nc.sync.dma_start(fn_sb[:], fn)
+            nc.sync.dma_start(out=xw[:], in_=x_words[0].rearrange("p n t -> p (n t)").bitcast(I32))
+            load_scales([nc.scalar] * 4, xs, x_scales)
+            load_scales([nc.scalar] * 3 + [nc.gpsimd], s1_raw, w1_scales)
+            make_identity(nc, ident[:])
+            nc.scalar.activation(warm[:], ident[:, 0:1], RELU)
+            nc.scalar.dma_start(out=w2_raw[:].bitcast(I32), in_=w2_words[0].bitcast(I32))
+            deal_words(0, w1_raw)
+        tables = ctx.enter_context(tc.tile_pool(name="tables", bufs=1))
+        cf = {}
+        for t in range(4):
+            for k, table in enumerate((cf1, cf2, cf3)):
+                cf[t, k] = tables.tile([P, D], F32, name="cf%d_%d" % (t, k), align_bytes=64)
+                nc.sync.dma_start(out=cf[t, k][:], in_=table.rearrange("(p t) c -> p t c", t=4)[:, t, :])
+        s2_raw = tables.tile([P, D], U8, name="s2_raw", align_bytes=64)
+        nc.gpsimd.memset(s2_raw[:].bitcast(I32), 0)
+        load_scales([nc.sync] * 4, s2_raw, w2_scales)
+
+        def deal_scales(i, raw):
+            nc.vector.tensor_copy(
+                out=s_sb[i][:].rearrange("p (t m) -> p t m", t=4),
+                in_=raw[:].rearrange("p (m t) -> p t m", t=4),
+            )
+
+        def product(i, acc, t, codes, scales):
+            nc.tensor.matmul_mx(
+                out=acc,
+                lhsT=w_sb[i][:, 2 * P * t : 2 * P * (t + 1)].bitcast(FP4X4),
+                lhsT_scale=s_sb[i][:, P * t : P * (t + 1)],
+                rhs=codes.bitcast(FP8X4),
+                rhs_scale=scales,
+                start=True,
+                stop=True,
+            )
+
+        picked_w = [tile("picked_w%d" % h, [P, PICK], U32) for h in range(S // PICK)]
+        picked_s = [tile("picked_s%d" % h, [P, PICK], U8) for h in range(S // PICK)]
+        for h in range(S // PICK):
+            nc.vector.tensor_copy(picked_s[h][:], xs[:].indirect(offs_sb[:, h * PICK // 16 : (h + 1) * PICK // 16]))
+        deal_scales(0, s1_raw)
+        for h in range(S // PICK):
+            nc.vector.tensor_copy(picked_w[h][:], xw[:].bitcast(U32).indirect(offs_sb[:, h * PICK // 16 : (h + 1) * PICK // 16]))
+        deal_words(1, w2_raw)
+
+        starts = [sum(CHUNKS[:c]) for c in range(len(CHUNKS))]
+        hinge = {}
+        for c, n in enumerate(CHUNKS):
+            h, lo = divmod(starts[c], PICK)
+            per = D // n
+            for t0 in range(0, 4, per):
+                y = bank("y", [P, per, n])
+                for e in range(per):
+                    product(0, y[:, e, :], t0 + e, picked_w[h][:, lo : lo + n], picked_s[h][:, lo : lo + n])
+                for k in range(3):
+                    r = tile("r%d_%d_%d" % (c, t0, k), [P, per, n], F32)
+                    nc.scalar.activation(r[:], y[:], RELU, bias=BIASES[k])
+                    for e in range(per):
+                        hinge[c, t0 + e, k] = r[:, e, :]
+
+        out_scales = tile("out_scales", [P, S], U8)
+        z_codes = {}
+        z_scales = {}
+        zq = {}
+        oq = {}
+        sums = {}
+        pairs = {}
+
+        def lookups(c, t, terms):
+            n = CHUNKS[c]
+            u, e = divmod(t, 2)
+            entries = fn_sb[:, starts[c] // 16 : (starts[c] + n) // 16]
+            if e == 0:
+                sums[c, u] = [bank("zsum", [P, 2, P]) for b in range(n // P)]
+            for k in range(3):
+                nc.vector.tensor_tensor(terms[:, k, :], cf[t, k][:].indirect(entries), hinge[c, t, k], MULT)
+                for b in range(n // P):
+                    nc.tensor.matmul(sums[c, u][b][:, e, :], lhsT=terms[:, k, b * P : (b + 1) * P], rhs=ident[:], is_transpose=True, start=(k == 0), stop=(k == 2))
+            if e == 1:
+                for b in range(n // P):
+                    pairs[c, u, b] = tile("pairs%d_%d_%d" % (c, u, b), [P, 2 * P], BF16)
+                    nc.scalar.copy(pairs[c, u, b][:].rearrange("s (p e) -> s p e", e=2), sums[c, u][b][:].rearrange("s e p -> s p e"))
+
+        def turn_back(c):
+            n = CHUNKS[c]
+            last = c == len(CHUNKS) - 1
+            zq[c] = tile("zq%d" % c, [P, 4 * n], BF16)
+            back = bank("back", [P, n // P, 2, P])
+            for u in range(2):
+                for b in range(n // P):
+                    nc.tensor.transpose(back[:, b, u, :], pairs[c, u, b][:].bitcast(F32), ident[:])
+            dst = zq[c][:].bitcast(F32).rearrange("p (b s u) -> p b s u", u=2, s=P)
+            src = back[:].rearrange("p b u s -> p b s u")
+            if last:
+                nc.vector.tensor_copy(dst, src)
+            else:
+                nc.scalar.copy(dst, src)
+
+        def quantise_z(c):
+            n = CHUNKS[c]
+            z_codes[c] = tile("z_codes%d" % c, [P, n], U32)
+            z_scales[c] = tile("z_scales%d" % c, [P, n], U8)
+            nc.vector.quantize_mx(out=z_codes[c][:].bitcast(FP8X4), scales=z_scales[c][:], in_=zq[c][:])
+
+        def second(c):
+            n = CHUNKS[c]
+            last = c == len(CHUNKS) - 1
+            cols = slice(starts[c], starts[c] + n)
+            res = tile("res%d" % c, [P, 4, n], F32)
+            oq[c] = tile("oq%d" % c, [P, 4 * n], BF16)
+            for b in range(n // P):
+                acc = bank("acc", [P, 4, P])
+                for t in range(4):
+                    product(1, acc[:, t, :], t, z_codes[c][:, b * P : (b + 1) * P], z_scales[c][:, b * P : (b + 1) * P])
+                dst = oq[c][:, 4 * P * b : 4 * P * (b + 1)].rearrange("p (s t) -> p s t", t=4)
+                src = acc[:].rearrange("p t s -> p s t")
+                if last:
+                    nc.vector.tensor_copy(dst, src)
+                else:
+                    nc.scalar.copy(dst, src)
+                nc.scalar.copy(res[:, :, b * P : (b + 1) * P], acc[:])
+            nc.sync.dma_start(out=out_0.rearrange("(p t) s -> p t s", t=4)[:, :, cols], in_=res[:])
+
+        def quantise_out(c):
+            n = CHUNKS[c]
+            cols = slice(starts[c], starts[c] + n)
+            codes = tile("o_codes%d" % c, [P, n], I32)
+            nc.vector.quantize_mx(out=codes[:].bitcast(FP8X4), scales=out_scales[:, cols], in_=oq[c][:])
+            nc.sync.dma_start(out=out_1[0].rearrange("p s t -> p (s t)").bitcast(I32)[:, cols], in_=codes[:])
+
+        room = tile("room0", [P, 4, 3, CHUNKS[0]], F32)
+        for t in range(4):
+            lookups(0, t, room[:, t])
+        turn_back(0)
+        room = tile("room1", [P, 3, 3, P], F32, tag="r0_2_2")
+        for t in range(3):
+            lookups(1, t, room[:, t])
+        deal_scales(1, s2_raw)
+        quantise_z(0)
+        second(0)
+        room = tile("room2", [P, 3, 3, P], F32, tag="zq0")
+        lookups(1, 3, room[:, 0])
+        turn_back(1)
+        lookups(2, 0, room[:, 1])
+        lookups(2, 1, room[:, 2])
+        quantise_z(1)
+        quantise_out(0)
+        second(1)
+        room = tile("room3", [P, 3, P], F32, tag="zq1")
+        lookups(2, 2, room[:])
+        room = tile("room4", [P, 3, P], F32, tag="oq0")
+        lookups(2, 3, room[:])
+        turn_back(2)
+        quantise_out(1)
+        quantise_z(2)
+        second(2)
+        quantise_out(2)
+        for q, queue in enumerate((nc.sync, nc.scalar, nc.sync, nc.scalar)):
+            queue.dma_start(out=out_2[0, 4 * q : 4 * q + 4, :].bitcast(I32), in_=out_scales[32 * q : 32 * q + 4, :].bitcast(I32))

@@ -13,6 +13,7 @@ FP8X4 = mybir.dt.float8_e4m3fn_x4
 FP4X4 = mybir.dt.float4_e2m1fn_x4
 RELU = mybir.ActivationFunctionType.Relu
 MULT = mybir.AluOpType.mult
+ADD = mybir.AluOpType.add
 
 P = 128
 T = 2048
@@ -21,7 +22,6 @@ D = 512
 FLOPS = 2 * 2 * D * D * S
 BIASES = (0.75, 0.0, -0.75)
 PICK = 256
-CHUNKS = (256, 128, 128)
 
 
 def tile_picked_kan8_none_po_kernel(tc, x_words, x_scales, w1_words, w1_scales, cf1, cf2, cf3, w2_words, w2_scales, offs, fn, out_0, out_1, out_2):
@@ -36,9 +36,9 @@ def tile_picked_kan8_none_po_kernel(tc, x_words, x_scales, w1_words, w1_scales, 
         def bank(name, shape):
             return ps.tile(shape, F32, name=name, tag="bank")
 
-        def load_scales(queues, plane, scales):
-            for q, queue in enumerate(queues):
-                queue.dma_start(out=plane[32 * q : 32 * q + 4, :].bitcast(I32), in_=scales[0, 4 * q : 4 * q + 4, :].bitcast(I32))
+        def load_scales(plane, scales):
+            for q in range(4):
+                nc.sync.dma_start(out=plane[32 * q : 32 * q + 4, :].bitcast(I32), in_=scales[0, 4 * q : 4 * q + 4, :].bitcast(I32))
 
         offs_sb = tile("offs_sb", [P, S // 16], U16)
         fn_sb = tile("fn_sb", [P, S // 16], U16)
@@ -50,43 +50,28 @@ def tile_picked_kan8_none_po_kernel(tc, x_words, x_scales, w1_words, w1_scales, 
         ident = tile("ident", [P, P], F32)
         warm = tile("warm", [P, 1], F32)
 
-        def deal_words(i, raw):
-            nc.vector.tensor_copy(
-                out=w_sb[i][:].rearrange("p (t m b) -> p t m b", t=4, b=2),
-                in_=raw[:].rearrange("p (m t b) -> p t m b", t=4, b=2),
-            )
-
+        w1_raw = tile("w1_raw", [P, 2 * D], U8)
+        w2_raw = tile("w2_raw", [P, 2 * D], U8)
+        s2_raw = tile("s2_raw", [P, D], U8)
         nc.vector.memset(xs[:].bitcast(I32), 0)
         nc.gpsimd.memset(s1_raw[:].bitcast(I32), 0)
+        nc.gpsimd.memset(s2_raw[:].bitcast(I32), 0)
+        make_identity(nc, ident[:])
+        nc.scalar.activation(warm[:], ident[:, 0:1], RELU)
 
-        with tc.tile_pool(name="head", bufs=1) as head:
-            w1_raw = head.tile([P, 2 * D], U8, name="w1_raw", align_bytes=64)
-            w2_raw = tile("w2_raw", [P, 2 * D], U8)
-            nc.sync.dma_start(offs_sb[:], offs)
-            nc.sync.dma_start(out=w1_raw[:].bitcast(I32), in_=w1_words[0].bitcast(I32))
-            nc.sync.dma_start(fn_sb[:], fn)
-            nc.sync.dma_start(out=xw[:], in_=x_words[0].rearrange("p n t -> p (n t)").bitcast(I32))
-            load_scales([nc.scalar] * 4, xs, x_scales)
-            load_scales([nc.scalar] * 3 + [nc.gpsimd], s1_raw, w1_scales)
-            make_identity(nc, ident[:])
-            nc.scalar.activation(warm[:], ident[:, 0:1], RELU)
-            nc.scalar.dma_start(out=w2_raw[:].bitcast(I32), in_=w2_words[0].bitcast(I32))
-            deal_words(0, w1_raw)
-        tables = ctx.enter_context(tc.tile_pool(name="tables", bufs=1))
+        nc.sync.dma_start(offs_sb[:], offs)
+        nc.sync.dma_start(out=w1_raw[:].bitcast(I32), in_=w1_words[0].bitcast(I32))
+        nc.sync.dma_start(out=w2_raw[:].bitcast(I32), in_=w2_words[0].bitcast(I32))
+        load_scales(xs, x_scales)
+        nc.sync.dma_start(out=xw[:], in_=x_words[0].rearrange("p n t -> p (n t)").bitcast(I32))
+        load_scales(s1_raw, w1_scales)
+        nc.sync.dma_start(fn_sb[:], fn)
         cf = {}
         for t in range(4):
             for k, table in enumerate((cf1, cf2, cf3)):
-                cf[t, k] = tables.tile([P, D], F32, name="cf%d_%d" % (t, k), align_bytes=64)
+                cf[t, k] = tile("cf%d_%d" % (t, k), [P, D], F32)
                 nc.sync.dma_start(out=cf[t, k][:], in_=table.rearrange("(p t) c -> p t c", t=4)[:, t, :])
-        s2_raw = tables.tile([P, D], U8, name="s2_raw", align_bytes=64)
-        nc.gpsimd.memset(s2_raw[:].bitcast(I32), 0)
-        load_scales([nc.sync] * 4, s2_raw, w2_scales)
-
-        def deal_scales(i, raw):
-            nc.vector.tensor_copy(
-                out=s_sb[i][:].rearrange("p (t m) -> p t m", t=4),
-                in_=raw[:].rearrange("p (m t) -> p t m", t=4),
-            )
+        load_scales(s2_raw, w2_scales)
 
         def product(i, acc, t, codes, scales):
             nc.tensor.matmul_mx(
@@ -99,126 +84,152 @@ def tile_picked_kan8_none_po_kernel(tc, x_words, x_scales, w1_words, w1_scales, 
                 stop=True,
             )
 
+        nc.vector.tensor_copy(
+            out=w_sb[0][:].rearrange("p (t m b) -> p t m b", t=4, b=2),
+            in_=w1_raw[:].rearrange("p (m t b) -> p t m b", t=4, b=2),
+        )
+        nc.vector.tensor_copy(
+            out=w_sb[1][:].rearrange("p (t m b) -> p t m b", t=4, b=2),
+            in_=w2_raw[:].rearrange("p (m t b) -> p t m b", t=4, b=2),
+        )
         picked_w = [tile("picked_w%d" % h, [P, PICK], U32) for h in range(S // PICK)]
         picked_s = [tile("picked_s%d" % h, [P, PICK], U8) for h in range(S // PICK)]
         for h in range(S // PICK):
             nc.vector.tensor_copy(picked_s[h][:], xs[:].indirect(offs_sb[:, h * PICK // 16 : (h + 1) * PICK // 16]))
-        deal_scales(0, s1_raw)
         for h in range(S // PICK):
             nc.vector.tensor_copy(picked_w[h][:], xw[:].bitcast(U32).indirect(offs_sb[:, h * PICK // 16 : (h + 1) * PICK // 16]))
-        deal_words(1, w2_raw)
+            nc.vector.tensor_copy(
+                out=s_sb[0][:].rearrange("p (t m) -> p t m", t=4)[:, 2 * h : 2 * h + 2],
+                in_=s1_raw[:].rearrange("p (m t) -> p t m", t=4)[:, 2 * h : 2 * h + 2],
+            )
 
-        starts = [sum(CHUNKS[:c]) for c in range(len(CHUNKS))]
         hinge = {}
-        for c, n in enumerate(CHUNKS):
-            h, lo = divmod(starts[c], PICK)
-            per = D // n
-            for t0 in range(0, 4, per):
-                y = bank("y", [P, per, n])
+        for c in range(2):
+            for t0, per in ((0, 1), (1, 1), (2, 2)) if c == 0 else ((0, 2), (2, 2)):
+                y = bank("y", [P, per, PICK])
                 for e in range(per):
-                    product(0, y[:, e, :], t0 + e, picked_w[h][:, lo : lo + n], picked_s[h][:, lo : lo + n])
+                    product(0, y[:, e, :], t0 + e, picked_w[c][:], picked_s[c][:])
                 for k in range(3):
-                    r = tile("r%d_%d_%d" % (c, t0, k), [P, per, n], F32)
+                    r = tile("r%d_%d_%d" % (c, t0, k), [P, per, PICK], F32)
                     nc.scalar.activation(r[:], y[:], RELU, bias=BIASES[k])
                     for e in range(per):
                         hinge[c, t0 + e, k] = r[:, e, :]
 
         out_scales = tile("out_scales", [P, S], U8)
-        z_codes = {}
-        z_scales = {}
-        zq = {}
-        oq = {}
+        out_rows = out_0.rearrange("(p t) s -> p t s", t=4)
+        out_words = out_1[0].rearrange("p s t -> p (s t)").bitcast(I32)
         sums = {}
         pairs = {}
 
-        def lookups(c, t, terms):
-            n = CHUNKS[c]
-            u, e = divmod(t, 2)
-            entries = fn_sb[:, starts[c] // 16 : (starts[c] + n) // 16]
-            if e == 0:
-                sums[c, u] = [bank("zsum", [P, 2, P]) for b in range(n // P)]
-            for k in range(3):
-                nc.vector.tensor_tensor(terms[:, k, :], cf[t, k][:].indirect(entries), hinge[c, t, k], MULT)
-                for b in range(n // P):
-                    nc.tensor.matmul(sums[c, u][b][:, e, :], lhsT=terms[:, k, b * P : (b + 1) * P], rhs=ident[:], is_transpose=True, start=(k == 0), stop=(k == 2))
-            if e == 1:
-                for b in range(n // P):
-                    pairs[c, u, b] = tile("pairs%d_%d_%d" % (c, u, b), [P, 2 * P], BF16)
-                    nc.scalar.copy(pairs[c, u, b][:].rearrange("s (p e) -> s p e", e=2), sums[c, u][b][:].rearrange("s e p -> s p e"))
+        def lookup(blocks, t, k, term):
+            u, h = divmod(t, 2)
+            first = blocks[0] * P
+            n = len(blocks) * P
+            c, lo = divmod(first, PICK)
+            entries = fn_sb[:, first // 16 : (first + n) // 16]
+            nc.vector.tensor_tensor(term, cf[t, k][:].indirect(entries), hinge[c, t, k][:, lo : lo + n], MULT)
+            for i, b in enumerate(blocks):
+                if b == 3:
+                    continue
+                if h == 0 and k == 0:
+                    sums[u, b] = bank("zsum", [P, 2, P])
+                nc.tensor.matmul(sums[u, b][:, h, :], lhsT=term[:, i * P : (i + 1) * P], rhs=ident[:], is_transpose=True, start=(k == 0), stop=(k == 2))
+                if h == 1 and k == 2:
+                    pairs[u, b] = tile("pairs%d_%d" % (u, b), [P, 2 * P], BF16)
+                    nc.scalar.copy(pairs[u, b][:].rearrange("s (p h) -> s p h", h=2), sums[u, b][:].rearrange("s h p -> s p h"))
 
-        def turn_back(c):
-            n = CHUNKS[c]
-            last = c == len(CHUNKS) - 1
-            zq[c] = tile("zq%d" % c, [P, 4 * n], BF16)
-            back = bank("back", [P, n // P, 2, P])
+        def lookups(name, steps, after=""):
+            room = tile(name, [P, P * sum(len(blocks) for blocks, t, k in steps)], F32, tag=after)
+            at = 0
+            for blocks, t, k in steps:
+                lookup(blocks, t, k, room[:, at : at + P * len(blocks)])
+                at = at + P * len(blocks)
+
+        def turn_back(blocks, words):
+            back = bank("back", [P, len(blocks), 2, P])
             for u in range(2):
-                for b in range(n // P):
-                    nc.tensor.transpose(back[:, b, u, :], pairs[c, u, b][:].bitcast(F32), ident[:])
-            dst = zq[c][:].bitcast(F32).rearrange("p (b s u) -> p b s u", u=2, s=P)
-            src = back[:].rearrange("p b u s -> p b s u")
+                for i, b in enumerate(blocks):
+                    nc.tensor.transpose(back[:, i, u, :], pairs[u, b][:].bitcast(F32), ident[:])
+            nc.scalar.copy(words.rearrange("p (b s u) -> p b s u", u=2, s=P), back[:].rearrange("p b u s -> p b s u"))
+
+        def second(blocks, zq, last):
+            n = len(blocks) * P
+            cols = slice(blocks[0] * P, blocks[0] * P + n)
+            codes = tile("z_codes%d" % blocks[0], [P, n], U32)
+            scales = tile("z_scales%d" % blocks[0], [P, n], U8)
+            nc.vector.quantize_mx(out=codes[:].bitcast(FP8X4), scales=scales[:], in_=zq)
+            oq = tile("oq%d" % blocks[0], [P, 4 * n], BF16)
             if last:
-                nc.vector.tensor_copy(dst, src)
-            else:
-                nc.scalar.copy(dst, src)
-
-        def quantise_z(c):
-            n = CHUNKS[c]
-            z_codes[c] = tile("z_codes%d" % c, [P, n], U32)
-            z_scales[c] = tile("z_scales%d" % c, [P, n], U8)
-            nc.vector.quantize_mx(out=z_codes[c][:].bitcast(FP8X4), scales=z_scales[c][:], in_=zq[c][:])
-
-        def second(c):
-            n = CHUNKS[c]
-            last = c == len(CHUNKS) - 1
-            cols = slice(starts[c], starts[c] + n)
-            res = tile("res%d" % c, [P, 4, n], F32)
-            oq[c] = tile("oq%d" % c, [P, 4 * n], BF16)
-            for b in range(n // P):
-                acc = bank("acc", [P, 4, P])
+                res = tile("res%d" % blocks[0], [P, 4, n], F32)
+                for half, copy in enumerate((nc.scalar.copy, nc.vector.tensor_copy)):
+                    acc = bank("acc", [P, 2, P])
+                    for e in range(2):
+                        product(1, acc[:, e, :], 2 * half + e, codes[:], scales[:])
+                    copy(res[:, 2 * half : 2 * half + 2, :], acc[:])
+                nc.sync.dma_start(out=out_rows[:, :, cols], in_=res[:])
+                nc.vector.tensor_copy(oq[:].rearrange("p (s i t) -> p s t i", t=4, i=4), res[:].rearrange("p t (s i) -> p s t i", i=4))
+                return oq
+            res = tile("res%d" % blocks[0], [P, 4, n], F32)
+            accs = [bank("acc", [P, 4, P]) for b in blocks]
+            for i, acc in enumerate(accs):
                 for t in range(4):
-                    product(1, acc[:, t, :], t, z_codes[c][:, b * P : (b + 1) * P], z_scales[c][:, b * P : (b + 1) * P])
-                dst = oq[c][:, 4 * P * b : 4 * P * (b + 1)].rearrange("p (s t) -> p s t", t=4)
-                src = acc[:].rearrange("p t s -> p s t")
-                if last:
-                    nc.vector.tensor_copy(dst, src)
-                else:
-                    nc.scalar.copy(dst, src)
-                nc.scalar.copy(res[:, :, b * P : (b + 1) * P], acc[:])
-            nc.sync.dma_start(out=out_0.rearrange("(p t) s -> p t s", t=4)[:, :, cols], in_=res[:])
+                    product(1, acc[:, t, :], t, codes[:, i * P : (i + 1) * P], scales[:, i * P : (i + 1) * P])
+                nc.scalar.copy(oq[:, 4 * P * i : 4 * P * (i + 1)].rearrange("p (s t) -> p s t", t=4), acc[:].rearrange("p t s -> p s t"))
+            for i, acc in enumerate(accs):
+                nc.scalar.copy(res[:, :, i * P : (i + 1) * P], acc[:])
+            nc.sync.dma_start(out=out_rows[:, :, cols], in_=res[:])
+            return oq
 
-        def quantise_out(c):
-            n = CHUNKS[c]
-            cols = slice(starts[c], starts[c] + n)
-            codes = tile("o_codes%d" % c, [P, n], I32)
-            nc.vector.quantize_mx(out=codes[:].bitcast(FP8X4), scales=out_scales[:, cols], in_=oq[c][:])
-            nc.sync.dma_start(out=out_1[0].rearrange("p s t -> p (s t)").bitcast(I32)[:, cols], in_=codes[:])
+        def hand_on(blocks, oq):
+            n = len(blocks) * P
+            cols = slice(blocks[0] * P, blocks[0] * P + n)
+            codes = tile("o_codes%d" % blocks[0], [P, n], I32)
+            nc.vector.quantize_mx(out=codes[:].bitcast(FP8X4), scales=out_scales[:, cols], in_=oq[:])
+            nc.sync.dma_start(out=out_words[:, cols], in_=codes[:])
 
-        room = tile("room0", [P, 4, 3, CHUNKS[0]], F32)
-        for t in range(4):
-            lookups(0, t, room[:, t])
-        turn_back(0)
-        room = tile("room1", [P, 3, 3, P], F32, tag="r0_2_2")
-        for t in range(3):
-            lookups(1, t, room[:, t])
-        deal_scales(1, s2_raw)
-        quantise_z(0)
-        second(0)
-        room = tile("room2", [P, 3, 3, P], F32, tag="zq0")
-        lookups(1, 3, room[:, 0])
-        turn_back(1)
-        lookups(2, 0, room[:, 1])
-        lookups(2, 1, room[:, 2])
-        quantise_z(1)
-        quantise_out(0)
-        second(1)
-        room = tile("room3", [P, 3, P], F32, tag="zq1")
-        lookups(2, 2, room[:])
-        room = tile("room4", [P, 3, P], F32, tag="oq0")
-        lookups(2, 3, room[:])
-        turn_back(2)
-        quantise_out(1)
-        quantise_z(2)
-        second(2)
-        quantise_out(2)
+        lookups("room0", [((0, 1), t, k) for t in range(4) for k in range(3)])
+        zq0 = tile("zq0", [P, 2 * PICK], F32)
+        turn_back((0, 1), zq0[:])
+        wide = tile("wide", [P, 2, 2, PICK], F32, tag="r0_2_2")
+        room1 = tile("room1", [P, 3, P], F32, tag="r0_2_1")
+        for t in range(2):
+            for k in range(2):
+                lookup((2, 3), t, k, wide[:, k, t, :])
+            lookup((2,), t, 2, room1[:, t, :])
+        lookup((2,), 2, 0, room1[:, 2, :])
+        nc.vector.tensor_copy(
+            out=s_sb[1][:].rearrange("p (t m) -> p t m", t=4),
+            in_=s2_raw[:].rearrange("p (m t) -> p t m", t=4),
+        )
+        oq0 = second((0, 1), zq0[:].bitcast(BF16), False)
+        room2 = tile("room2", [P, 13, P], F32, tag="zq0")
+        for i, (t, k) in enumerate(((2, 1), (2, 2), (3, 0), (3, 1), (3, 2))):
+            lookup((2,), t, k, room2[:, i, :])
+        late = room2[:, 5:9, :]
+        third = room2[:, 9:13, :]
+        zq2 = third[:, 2:4, :].rearrange("p t s -> p (t s)")
+        turn_back((2,), zq2)
+        for k in range(2):
+            for t in (2, 3):
+                lookup((3,), t, k, late[:, 2 * k + t - 2, :])
+        hand_on((0, 1), oq0)
+        part = tile("part", [P, 4, P], F32, tag="oq0")
+        nc.vector.tensor_tensor(part[:, 0:2, :], wide[:, 0, :, P:], wide[:, 1, :, P:], ADD)
+        nc.vector.tensor_tensor(part[:, 2:4, :], late[:, 0:2, :], late[:, 2:4, :], ADD)
+        for t in range(2):
+            lookup((3,), t, 2, third[:, t, :])
+        oq2 = second((2,), zq2.bitcast(BF16), False)
+        for t in (2, 3):
+            lookup((3,), t, 2, third[:, t, :])
+        zq3 = tile("zq3", [P, 4 * P], BF16)
+        nc.vector.tensor_tensor(
+            zq3[:].rearrange("p (s i t) -> p s t i", t=4, i=4),
+            part[:].rearrange("p t (s i) -> p s t i", i=4),
+            third.rearrange("p t (s i) -> p s t i", i=4),
+            ADD,
+        )
+        oq3 = second((3,), zq3[:], True)
+        hand_on((2,), oq2)
+        hand_on((3,), oq3)
         for q, queue in enumerate((nc.sync, nc.scalar, nc.sync, nc.scalar)):
             queue.dma_start(out=out_2[0, 4 * q : 4 * q + 4, :].bitcast(I32), in_=out_scales[32 * q : 32 * q + 4, :].bitcast(I32))

@@ -61,10 +61,10 @@ def tile_picked_kan8_none_po_kernel(tc, x_words, x_scales, w1_words, w1_scales, 
 
         nc.sync.dma_start(offs_sb[:], offs)
         nc.sync.dma_start(out=w1_raw[:].bitcast(I32), in_=w1_words[0].bitcast(I32))
-        nc.sync.dma_start(out=w2_raw[:].bitcast(I32), in_=w2_words[0].bitcast(I32))
         load_scales(xs, x_scales)
         nc.sync.dma_start(out=xw[:], in_=x_words[0].rearrange("p n t -> p (n t)").bitcast(I32))
         load_scales(s1_raw, w1_scales)
+        nc.sync.dma_start(out=w2_raw[:].bitcast(I32), in_=w2_words[0].bitcast(I32))
         nc.sync.dma_start(fn_sb[:], fn)
         cf = {}
         for t in range(4):
@@ -88,10 +88,6 @@ def tile_picked_kan8_none_po_kernel(tc, x_words, x_scales, w1_words, w1_scales, 
             out=w_sb[0][:].rearrange("p (t m b) -> p t m b", t=4, b=2),
             in_=w1_raw[:].rearrange("p (m t b) -> p t m b", t=4, b=2),
         )
-        nc.vector.tensor_copy(
-            out=w_sb[1][:].rearrange("p (t m b) -> p t m b", t=4, b=2),
-            in_=w2_raw[:].rearrange("p (m t b) -> p t m b", t=4, b=2),
-        )
         picked_w = [tile("picked_w%d" % h, [P, PICK], U32) for h in range(S // PICK)]
         picked_s = [tile("picked_s%d" % h, [P, PICK], U8) for h in range(S // PICK)]
         for h in range(S // PICK):
@@ -102,6 +98,10 @@ def tile_picked_kan8_none_po_kernel(tc, x_words, x_scales, w1_words, w1_scales, 
                 out=s_sb[0][:].rearrange("p (t m) -> p t m", t=4)[:, 2 * h : 2 * h + 2],
                 in_=s1_raw[:].rearrange("p (m t) -> p t m", t=4)[:, 2 * h : 2 * h + 2],
             )
+        nc.vector.tensor_copy(
+            out=w_sb[1][:].rearrange("p (t m b) -> p t m b", t=4, b=2),
+            in_=w2_raw[:].rearrange("p (m t b) -> p t m b", t=4, b=2),
+        )
 
         hinge = {}
         for c in range(2):
@@ -129,7 +129,7 @@ def tile_picked_kan8_none_po_kernel(tc, x_words, x_scales, w1_words, w1_scales, 
             entries = fn_sb[:, first // 16 : (first + n) // 16]
             nc.vector.tensor_tensor(term, cf[t, k][:].indirect(entries), hinge[c, t, k][:, lo : lo + n], MULT)
             for i, b in enumerate(blocks):
-                if b == 3:
+                if b == 3 and u == 1:
                     continue
                 if h == 0 and k == 0:
                     sums[u, b] = bank("zsum", [P, 2, P])
@@ -160,25 +160,29 @@ def tile_picked_kan8_none_po_kernel(tc, x_words, x_scales, w1_words, w1_scales, 
             nc.vector.quantize_mx(out=codes[:].bitcast(FP8X4), scales=scales[:], in_=zq)
             oq = tile("oq%d" % blocks[0], [P, 4 * n], BF16)
             if last:
-                res = tile("res%d" % blocks[0], [P, 4, n], F32)
                 for half, copy in enumerate((nc.scalar.copy, nc.vector.tensor_copy)):
+                    planes = slice(2 * half, 2 * half + 2)
                     acc = bank("acc", [P, 2, P])
                     for e in range(2):
                         product(1, acc[:, e, :], 2 * half + e, codes[:], scales[:])
-                    copy(res[:, 2 * half : 2 * half + 2, :], acc[:])
-                nc.sync.dma_start(out=out_rows[:, :, cols], in_=res[:])
-                nc.vector.tensor_copy(oq[:].rearrange("p (s i t) -> p s t i", t=4, i=4), res[:].rearrange("p t (s i) -> p s t i", i=4))
+                    copy(oq[:].rearrange("p (s t) -> p s t", t=4)[:, :, planes], acc[:].rearrange("p t s -> p s t"))
+                    res = tile("res_half%d" % half, [P, 2, n], F32)
+                    nc.scalar.copy(res[:], acc[:])
+                    nc.sync.dma_start(out=out_rows[:, planes, cols], in_=res[:])
                 return oq
-            res = tile("res%d" % blocks[0], [P, 4, n], F32)
             accs = [bank("acc", [P, 4, P]) for b in blocks]
             for i, acc in enumerate(accs):
                 for t in range(4):
                     product(1, acc[:, t, :], t, codes[:, i * P : (i + 1) * P], scales[:, i * P : (i + 1) * P])
                 nc.scalar.copy(oq[:, 4 * P * i : 4 * P * (i + 1)].rearrange("p (s t) -> p s t", t=4), acc[:].rearrange("p t s -> p s t"))
+            return oq, accs
+
+        def store(blocks, accs):
+            n = len(blocks) * P
+            res = tile("res%d" % blocks[0], [P, 4, n], F32)
             for i, acc in enumerate(accs):
                 nc.scalar.copy(res[:, :, i * P : (i + 1) * P], acc[:])
-            nc.sync.dma_start(out=out_rows[:, :, cols], in_=res[:])
-            return oq
+            nc.sync.dma_start(out=out_rows[:, :, blocks[0] * P : blocks[0] * P + n], in_=res[:])
 
         def hand_on(blocks, oq):
             n = len(blocks) * P
@@ -190,46 +194,43 @@ def tile_picked_kan8_none_po_kernel(tc, x_words, x_scales, w1_words, w1_scales, 
         lookups("room0", [((0, 1), t, k) for t in range(4) for k in range(3)])
         zq0 = tile("zq0", [P, 2 * PICK], F32)
         turn_back((0, 1), zq0[:])
-        wide = tile("wide", [P, 2, 2, PICK], F32, tag="r0_2_2")
-        room1 = tile("room1", [P, 3, P], F32, tag="r0_2_1")
-        for t in range(2):
-            for k in range(2):
-                lookup((2, 3), t, k, wide[:, k, t, :])
-            lookup((2,), t, 2, room1[:, t, :])
-        lookup((2,), 2, 0, room1[:, 2, :])
+        lookups("room1", [((2, 3), 0, k) for k in range(3)] + [((2,), 1, k) for k in range(3)] + [((2,), 2, k) for k in range(2)], after="r0_2_2")
         nc.vector.tensor_copy(
             out=s_sb[1][:].rearrange("p (t m) -> p t m", t=4),
             in_=s2_raw[:].rearrange("p (m t) -> p t m", t=4),
         )
-        oq0 = second((0, 1), zq0[:].bitcast(BF16), False)
-        room2 = tile("room2", [P, 13, P], F32, tag="zq0")
-        for i, (t, k) in enumerate(((2, 1), (2, 2), (3, 0), (3, 1), (3, 2))):
+        oq0, accs0 = second((0, 1), zq0[:].bitcast(BF16), False)
+        room2 = tile("room2", [P, 15, P], F32, tag="zq0")
+        for i, (t, k) in enumerate(((2, 2), (3, 0), (3, 1), (3, 2))):
             lookup((2,), t, k, room2[:, i, :])
-        late = room2[:, 5:9, :]
-        third = room2[:, 9:13, :]
-        zq2 = third[:, 2:4, :].rearrange("p t s -> p (t s)")
+        part = room2[:, 13:15, :]
+        zq2 = part.rearrange("p t s -> p (t s)")
         turn_back((2,), zq2)
+        for k in range(3):
+            lookup((3,), 1, k, room2[:, 4 + k, :])
+        zq3 = tile("zq3", [P, 4 * P], BF16)
+        back = bank("back", [P, P])
+        nc.tensor.transpose(back[:], pairs[0, 3][:].bitcast(F32), ident[:])
+        nc.scalar.copy(zq3[:].bitcast(F32).rearrange("p (s u) -> p s u", u=2)[:, :, 0], back[:])
+        store((0, 1), accs0)
+        late = room2[:, 7:13, :]
         for k in range(2):
             for t in (2, 3):
                 lookup((3,), t, k, late[:, 2 * k + t - 2, :])
-        hand_on((0, 1), oq0)
-        part = tile("part", [P, 4, P], F32, tag="oq0")
-        nc.vector.tensor_tensor(part[:, 0:2, :], wide[:, 0, :, P:], wide[:, 1, :, P:], ADD)
-        nc.vector.tensor_tensor(part[:, 2:4, :], late[:, 0:2, :], late[:, 2:4, :], ADD)
-        for t in range(2):
-            lookup((3,), t, 2, third[:, t, :])
-        oq2 = second((2,), zq2.bitcast(BF16), False)
-        for t in (2, 3):
-            lookup((3,), t, 2, third[:, t, :])
-        zq3 = tile("zq3", [P, 4 * P], BF16)
+        lookup((3,), 2, 2, late[:, 4, :])
+        oq2, accs2 = second((2,), zq2.bitcast(BF16), False)
+        store((2,), accs2)
+        nc.vector.tensor_tensor(part, late[:, 0:2, :], late[:, 2:4, :], ADD)
+        lookup((3,), 3, 2, late[:, 5, :])
         nc.vector.tensor_tensor(
-            zq3[:].rearrange("p (s i t) -> p s t i", t=4, i=4),
-            part[:].rearrange("p t (s i) -> p s t i", i=4),
-            third.rearrange("p t (s i) -> p s t i", i=4),
+            zq3[:].rearrange("p (s t) -> p s t", t=4)[:, :, 2:4],
+            part.rearrange("p t s -> p s t"),
+            late[:, 4:6, :].rearrange("p t s -> p s t"),
             ADD,
         )
         oq3 = second((3,), zq3[:], True)
-        hand_on((2,), oq2)
         hand_on((3,), oq3)
+        hand_on((0, 1), oq0)
+        hand_on((2,), oq2)
         for q, queue in enumerate((nc.sync, nc.scalar, nc.sync, nc.scalar)):
             queue.dma_start(out=out_2[0, 4 * q : 4 * q + 4, :].bitcast(I32), in_=out_scales[32 * q : 32 * q + 4, :].bitcast(I32))

@@ -16,221 +16,267 @@ MULT = mybir.AluOpType.mult
 ADD = mybir.AluOpType.add
 
 P = 128
-T = 2048
-S = 512
-D = 512
-FLOPS = 2 * 2 * D * D * S
-BIASES = (0.75, 0.0, -0.75)
-PICK = 256
+TOKENS = 2048
+PICKED = 512
+WIDTH = 512
+HALF = 256
+PLANES = 4
+KNOTS = 3
+KNOT = 0.75
+GROUP = 16
+PSUM_BANKS = 8
+LAST = 3
+EARLY = 8
+FLOPS = 2 * 2 * WIDTH * WIDTH * PICKED
 
 
-def tile_picked_kan8_none_po_kernel(tc, x_words, x_scales, w1_words, w1_scales, cf1, cf2, cf3, w2_words, w2_scales, offs, fn, out_0, out_1, out_2):
+def tile_picked_kan8_none_po_kernel(
+    tc, x_words, x_scales, w1_words, w1_scales, cf1, cf2, cf3, w2_words, w2_scales, offs, fn, out_0, out_1, out_2
+):
     nc = tc.nc
     with ExitStack() as ctx:
-        sb = ctx.enter_context(tc.tile_pool(name="sb", bufs=1))
-        ps = ctx.enter_context(tc.psum_pool(name="ps", bufs=8))
+        sbuf = ctx.enter_context(tc.tile_pool(name="sbuf", bufs=1))
+        psum = ctx.enter_context(tc.psum_pool(name="psum", bufs=PSUM_BANKS))
 
-        def tile(name, shape, dtype, tag=""):
-            return sb.tile(shape, dtype, name=name, tag=tag or name, align_bytes=64)
+        def tile(name, shape, dtype, reuses=""):
+            return sbuf.tile(shape, dtype, name=name, tag=reuses or name, align_bytes=64)
 
         def bank(name, shape):
-            return ps.tile(shape, F32, name=name, tag="bank")
+            return psum.tile(shape, F32, name=name, tag="bank")
 
-        def load_scales(plane, scales):
+        def load_scale_rows(dst, scales):
             for q in range(4):
-                nc.sync.dma_start(out=plane[32 * q : 32 * q + 4, :].bitcast(I32), in_=scales[0, 4 * q : 4 * q + 4, :].bitcast(I32))
+                nc.sync.dma_start(
+                    out=dst[32 * q : 32 * q + 4, :].bitcast(I32), in_=scales[0, 4 * q : 4 * q + 4, :].bitcast(I32)
+                )
 
-        offs_sb = tile("offs_sb", [P, S // 16], U16)
-        fn_sb = tile("fn_sb", [P, S // 16], U16)
-        xw = tile("xw", [P, T], I32)
-        xs = tile("xs", [P, T], U8)
-        s1_raw = tile("s1_raw", [P, D], U8)
-        w_sb = [tile("w_sb%d" % i, [P, 2 * D], U8) for i in range(2)]
-        s_sb = [tile("s_sb%d" % i, [P, D], U8) for i in range(2)]
+        def deal_words(engine, dst, src):
+            engine.tensor_copy(
+                out=dst[:].rearrange("p (t m b) -> p t m b", t=PLANES, b=2),
+                in_=src[:].rearrange("p (m t b) -> p t m b", t=PLANES, b=2),
+            )
+
+        def deal_scales(dst, src):
+            nc.vector.tensor_copy(
+                out=dst[:].rearrange("p (t m) -> p t m", t=PLANES),
+                in_=src[:].rearrange("p (m t) -> p t m", t=PLANES),
+            )
+
+        def entries(list_tile, first, count):
+            return list_tile[:, first // GROUP : (first + count) // GROUP]
+
+        offs_sb = tile("offs_sb", [P, PICKED // GROUP], U16)
+        fn_sb = tile("fn_sb", [P, PICKED // GROUP], U16)
+        x_words_sb = tile("x_words_sb", [P, TOKENS], I32)
+        x_scales_sb = tile("x_scales_sb", [P, TOKENS], U8)
+        w1_scales_sb = tile("w1_scales_sb", [P, WIDTH], U8)
+        dealt_words = [tile("dealt_words%d" % layer, [P, 2 * WIDTH], U8) for layer in range(2)]
+        dealt_scales = [tile("dealt_scales%d" % layer, [P, WIDTH], U8) for layer in range(2)]
         ident = tile("ident", [P, P], F32)
-        warm = tile("warm", [P, 1], F32)
+        knot_column = tile("knot_column", [P, 1], F32)
+        w1_words_sb = tile("w1_words_sb", [P, 2 * WIDTH], U8)
+        w2_words_sb = tile("w2_words_sb", [P, 2 * WIDTH], U8)
+        w2_scales_sb = tile("w2_scales_sb", [P, WIDTH], U8)
 
-        w1_raw = tile("w1_raw", [P, 2 * D], U8)
-        w2_raw = tile("w2_raw", [P, 2 * D], U8)
-        s2_raw = tile("s2_raw", [P, D], U8)
-        nc.vector.memset(xs[:].bitcast(I32), 0)
-        nc.gpsimd.memset(s1_raw[:].bitcast(I32), 0)
-        nc.gpsimd.memset(s2_raw[:].bitcast(I32), 0)
+        nc.vector.memset(x_scales_sb[:].bitcast(I32), 0)
+        nc.gpsimd.memset(w1_scales_sb[:].bitcast(I32), 0)
+        nc.gpsimd.memset(w2_scales_sb[:].bitcast(I32), 0)
         make_identity(nc, ident[:])
-        nc.scalar.activation(warm[:], ident[:, 0:1], RELU)
+        nc.scalar.activation(knot_column[:], ident[:, 0:1], RELU, bias=KNOT, scale=0.0)
+        knot_bias = (knot_column[:], 0.0, -KNOT)
 
         nc.sync.dma_start(offs_sb[:], offs)
-        nc.sync.dma_start(out=w1_raw[:].bitcast(I32), in_=w1_words[0].bitcast(I32))
-        load_scales(xs, x_scales)
-        nc.sync.dma_start(out=xw[:], in_=x_words[0].rearrange("p n t -> p (n t)").bitcast(I32))
-        load_scales(s1_raw, w1_scales)
-        nc.sync.dma_start(out=w2_raw[:].bitcast(I32), in_=w2_words[0].bitcast(I32))
+        nc.sync.dma_start(out=w1_words_sb[:].bitcast(I32), in_=w1_words[0].bitcast(I32))
+        nc.sync.dma_start(out=w2_words_sb[:].bitcast(I32), in_=w2_words[0].bitcast(I32))
+        load_scale_rows(x_scales_sb, x_scales)
+        nc.sync.dma_start(out=x_words_sb[:], in_=x_words[0].rearrange("p n t -> p (n t)").bitcast(I32))
+        load_scale_rows(w1_scales_sb, w1_scales)
         nc.sync.dma_start(fn_sb[:], fn)
-        cf = {}
-        for t in range(4):
-            for k, table in enumerate((cf1, cf2, cf3)):
-                cf[t, k] = tile("cf%d_%d" % (t, k), [P, D], F32)
-                nc.sync.dma_start(out=cf[t, k][:], in_=table.rearrange("(p t) c -> p t c", t=4)[:, t, :])
-        load_scales(s2_raw, w2_scales)
+        table = {}
+        for t in range(PLANES):
+            for k, cf in enumerate((cf1, cf2, cf3)):
+                table[t, k] = tile("table%d_%d" % (t, k), [P, WIDTH], F32)
+                nc.sync.dma_start(out=table[t, k][:], in_=cf.rearrange("(p t) c -> p t c", t=PLANES)[:, t, :])
+        load_scale_rows(w2_scales_sb, w2_scales)
 
-        def product(i, acc, t, codes, scales):
+        def product(layer, acc, t, codes, scales):
             nc.tensor.matmul_mx(
                 out=acc,
-                lhsT=w_sb[i][:, 2 * P * t : 2 * P * (t + 1)].bitcast(FP4X4),
-                lhsT_scale=s_sb[i][:, P * t : P * (t + 1)],
+                lhsT=dealt_words[layer][:, 2 * P * t : 2 * P * (t + 1)].bitcast(FP4X4),
+                lhsT_scale=dealt_scales[layer][:, P * t : P * (t + 1)],
                 rhs=codes.bitcast(FP8X4),
                 rhs_scale=scales,
                 start=True,
                 stop=True,
             )
 
-        nc.vector.tensor_copy(
-            out=w_sb[0][:].rearrange("p (t m b) -> p t m b", t=4, b=2),
-            in_=w1_raw[:].rearrange("p (m t b) -> p t m b", t=4, b=2),
-        )
-        picked_w = [tile("picked_w%d" % h, [P, PICK], U32) for h in range(S // PICK)]
-        picked_s = [tile("picked_s%d" % h, [P, PICK], U8) for h in range(S // PICK)]
-        for h in range(S // PICK):
-            nc.vector.tensor_copy(picked_s[h][:], xs[:].indirect(offs_sb[:, h * PICK // 16 : (h + 1) * PICK // 16]))
-        for h in range(S // PICK):
-            nc.vector.tensor_copy(picked_w[h][:], xw[:].bitcast(U32).indirect(offs_sb[:, h * PICK // 16 : (h + 1) * PICK // 16]))
-            nc.vector.tensor_copy(
-                out=s_sb[0][:].rearrange("p (t m) -> p t m", t=4)[:, 2 * h : 2 * h + 2],
-                in_=s1_raw[:].rearrange("p (m t) -> p t m", t=4)[:, 2 * h : 2 * h + 2],
-            )
-        nc.vector.tensor_copy(
-            out=w_sb[1][:].rearrange("p (t m b) -> p t m b", t=4, b=2),
-            in_=w2_raw[:].rearrange("p (m t b) -> p t m b", t=4, b=2),
-        )
+        deal_words(nc.vector, dealt_words[0], w1_words_sb)
+        deal_words(nc.gpsimd, dealt_words[1], w2_words_sb)
+        picked_scales = [tile("picked_scales%d" % half, [P, HALF], U8) for half in range(2)]
+        for half in range(2):
+            nc.vector.tensor_copy(picked_scales[half][:], x_scales_sb[:].indirect(entries(offs_sb, half * HALF, HALF)))
+        token_words = x_words_sb[:].bitcast(U32)
+        picked_words = [tile("picked_words0", [P, HALF], U32)]
+        nc.vector.tensor_copy(picked_words[0][:], token_words.indirect(entries(offs_sb, 0, HALF)))
+        deal_scales(dealt_scales[0], w1_scales_sb)
+        picked_words.append(tile("picked_words1", [P, HALF], U32, reuses="w1_scales_sb"))
+        nc.vector.tensor_copy(picked_words[1][:], token_words.indirect(entries(offs_sb, HALF, HALF)))
 
         hinge = {}
-        for c in range(2):
-            for t0, per in ((0, 1), (1, 1), (2, 2)) if c == 0 else ((0, 2), (2, 2)):
-                y = bank("y", [P, per, PICK])
-                for e in range(per):
-                    product(0, y[:, e, :], t0 + e, picked_w[c][:], picked_s[c][:])
-                for k in range(3):
-                    r = tile("r%d_%d_%d" % (c, t0, k), [P, per, PICK], F32)
-                    nc.scalar.activation(r[:], y[:], RELU, bias=BIASES[k])
-                    for e in range(per):
-                        hinge[c, t0 + e, k] = r[:, e, :]
+        banked_planes = (((0,), (1,), (2, 3)), ((0, 1), (2, 3)))
+        for half in range(2):
+            for planes in banked_planes[half]:
+                y = bank("y", [P, len(planes), HALF])
+                for i, t in enumerate(planes):
+                    product(0, y[:, i, :], t, picked_words[half][:], picked_scales[half][:])
+                for k in range(KNOTS):
+                    relu = tile("hinge%d_%d_%d" % (half, planes[0], k), [P, len(planes), HALF], F32)
+                    nc.scalar.activation(relu[:], y[:], RELU, bias=knot_bias[k])
+                    for i, t in enumerate(planes):
+                        hinge[half, t, k] = relu[:, i, :]
 
-        out_scales = tile("out_scales", [P, S], U8)
-        out_rows = out_0.rearrange("(p t) s -> p t s", t=4)
+        out_scales = tile("out_scales", [P, PICKED], U8)
+        out_rows = out_0.rearrange("(p t) s -> p t s", t=PLANES)
         out_words = out_1[0].rearrange("p s t -> p (s t)").bitcast(I32)
         sums = {}
         pairs = {}
 
-        def lookup(blocks, t, k, term):
-            u, h = divmod(t, 2)
-            first = blocks[0] * P
-            n = len(blocks) * P
-            c, lo = divmod(first, PICK)
-            entries = fn_sb[:, first // 16 : (first + n) // 16]
-            nc.vector.tensor_tensor(term, cf[t, k][:].indirect(entries), hinge[c, t, k][:, lo : lo + n], MULT)
-            for i, b in enumerate(blocks):
-                if b == 3 and u == 1:
-                    continue
-                if h == 0 and k == 0:
-                    sums[u, b] = bank("zsum", [P, 2, P])
-                nc.tensor.matmul(sums[u, b][:, h, :], lhsT=term[:, i * P : (i + 1) * P], rhs=ident[:], is_transpose=True, start=(k == 0), stop=(k == 2))
-                if h == 1 and k == 2:
-                    pairs[u, b] = tile("pairs%d_%d" % (u, b), [P, 2 * P], BF16)
-                    nc.scalar.copy(pairs[u, b][:].rearrange("s (p h) -> s p h", h=2), sums[u, b][:].rearrange("s h p -> s p h"))
+        def columns(blocks):
+            return slice(blocks[0] * P, (blocks[-1] + 1) * P)
 
-        def lookups(name, steps, after=""):
-            room = tile(name, [P, P * sum(len(blocks) for blocks, t, k in steps)], F32, tag=after)
-            at = 0
+        def look_up(blocks, t, k, term):
+            half, first = divmod(blocks[0] * P, HALF)
+            count = len(blocks) * P
+            slopes = table[t, k][:].indirect(entries(fn_sb, blocks[0] * P, count))
+            nc.vector.tensor_tensor(term, slopes, hinge[half, t, k][:, first : first + count], MULT)
+
+        def add_up(blocks, t, k, term):
+            u, e = divmod(t, 2)
+            for i, b in enumerate(blocks):
+                if e == 0 and k == 0:
+                    sums[u, b] = bank("sums", [P, 2, P])
+                nc.tensor.matmul(
+                    sums[u, b][:, e, :],
+                    lhsT=term[:, i * P : (i + 1) * P],
+                    rhs=ident[:],
+                    is_transpose=True,
+                    start=(k == 0),
+                    stop=(k == KNOTS - 1),
+                )
+                if e == 1 and k == KNOTS - 1:
+                    pairs[u, b] = tile("pairs%d_%d" % (u, b), [P, 2 * P], BF16)
+                    nc.scalar.copy(
+                        pairs[u, b][:].rearrange("s (p e) -> s p e", e=2), sums[u, b][:].rearrange("s e p -> s p e")
+                    )
+
+        def look_up_and_add(steps, terms):
+            first = 0
             for blocks, t, k in steps:
-                lookup(blocks, t, k, room[:, at : at + P * len(blocks)])
-                at = at + P * len(blocks)
+                term = terms[:, first : first + P * len(blocks)]
+                look_up(blocks, t, k, term)
+                add_up(blocks, t, k, term)
+                first = first + P * len(blocks)
 
         def turn_back(blocks, words):
             back = bank("back", [P, len(blocks), 2, P])
             for u in range(2):
                 for i, b in enumerate(blocks):
                     nc.tensor.transpose(back[:, i, u, :], pairs[u, b][:].bitcast(F32), ident[:])
-            nc.scalar.copy(words.rearrange("p (b s u) -> p b s u", u=2, s=P), back[:].rearrange("p b u s -> p b s u"))
+            nc.scalar.copy(
+                words.rearrange("p (b s u) -> p b s u", u=2, s=P), back[:].rearrange("p b u s -> p b s u")
+            )
 
-        def second(blocks, zq, last):
-            n = len(blocks) * P
-            cols = slice(blocks[0] * P, blocks[0] * P + n)
-            codes = tile("z_codes%d" % blocks[0], [P, n], U32)
-            scales = tile("z_scales%d" % blocks[0], [P, n], U8)
-            nc.vector.quantize_mx(out=codes[:].bitcast(FP8X4), scales=scales[:], in_=zq)
-            oq = tile("oq%d" % blocks[0], [P, 4 * n], BF16)
-            if last:
-                for half, copy in enumerate((nc.scalar.copy, nc.vector.tensor_copy)):
-                    planes = slice(2 * half, 2 * half + 2)
-                    acc = bank("acc", [P, 2, P])
-                    for e in range(2):
-                        product(1, acc[:, e, :], 2 * half + e, codes[:], scales[:])
-                    copy(oq[:].rearrange("p (s t) -> p s t", t=4)[:, :, planes], acc[:].rearrange("p t s -> p s t"))
-                    res = tile("res_half%d" % half, [P, 2, n], F32)
-                    nc.scalar.copy(res[:], acc[:])
-                    nc.sync.dma_start(out=out_rows[:, planes, cols], in_=res[:])
-                return oq
-            accs = [bank("acc", [P, 4, P]) for b in blocks]
+        def quantise_z(blocks, z):
+            codes = tile("z_codes%d" % blocks[0], [P, len(blocks) * P], U32)
+            scales = tile("z_scales%d" % blocks[0], [P, len(blocks) * P], U8)
+            nc.vector.quantize_mx(out=codes[:].bitcast(FP8X4), scales=scales[:], in_=z)
+            return codes, scales
+
+        def second_layer(blocks, z):
+            codes, scales = quantise_z(blocks, z)
+            rounded = tile("rounded%d" % blocks[0], [P, PLANES * P * len(blocks)], BF16)
+            accs = [bank("acc", [P, PLANES, P]) for b in blocks]
             for i, acc in enumerate(accs):
-                for t in range(4):
+                for t in range(PLANES):
                     product(1, acc[:, t, :], t, codes[:, i * P : (i + 1) * P], scales[:, i * P : (i + 1) * P])
-                nc.scalar.copy(oq[:, 4 * P * i : 4 * P * (i + 1)].rearrange("p (s t) -> p s t", t=4), acc[:].rearrange("p t s -> p s t"))
-            return oq, accs
+                nc.scalar.copy(
+                    rounded[:, PLANES * P * i : PLANES * P * (i + 1)].rearrange("p (s t) -> p s t", t=PLANES),
+                    acc[:].rearrange("p t s -> p s t"),
+                )
+            return rounded, accs
 
-        def store(blocks, accs):
-            n = len(blocks) * P
-            res = tile("res%d" % blocks[0], [P, 4, n], F32)
+        def store_result(blocks, accs):
+            result = tile("result%d" % blocks[0], [P, PLANES, len(blocks) * P], F32)
             for i, acc in enumerate(accs):
-                nc.scalar.copy(res[:, :, i * P : (i + 1) * P], acc[:])
-            nc.sync.dma_start(out=out_rows[:, :, blocks[0] * P : blocks[0] * P + n], in_=res[:])
+                nc.scalar.copy(result[:, :, i * P : (i + 1) * P], acc[:])
+            nc.sync.dma_start(out=out_rows[:, :, columns(blocks)], in_=result[:])
 
-        def hand_on(blocks, oq):
-            n = len(blocks) * P
-            cols = slice(blocks[0] * P, blocks[0] * P + n)
-            codes = tile("o_codes%d" % blocks[0], [P, n], I32)
-            nc.vector.quantize_mx(out=codes[:].bitcast(FP8X4), scales=out_scales[:, cols], in_=oq[:])
-            nc.sync.dma_start(out=out_words[:, cols], in_=codes[:])
+        def hand_on(blocks, rounded):
+            codes = tile("out_codes%d" % blocks[0], [P, len(blocks) * P], I32)
+            nc.vector.quantize_mx(out=codes[:].bitcast(FP8X4), scales=out_scales[:, columns(blocks)], in_=rounded[:])
+            nc.sync.dma_start(out=out_words[:, columns(blocks)], in_=codes[:])
 
-        lookups("room0", [((0, 1), t, k) for t in range(4) for k in range(3)])
-        zq0 = tile("zq0", [P, 2 * PICK], F32)
-        turn_back((0, 1), zq0[:])
-        lookups("room1", [((2, 3), 0, k) for k in range(3)] + [((2,), 1, k) for k in range(3)] + [((2,), 2, k) for k in range(2)], after="r0_2_2")
-        nc.vector.tensor_copy(
-            out=s_sb[1][:].rearrange("p (t m) -> p t m", t=4),
-            in_=s2_raw[:].rearrange("p (m t) -> p t m", t=4),
-        )
-        oq0, accs0 = second((0, 1), zq0[:].bitcast(BF16), False)
-        room2 = tile("room2", [P, 15, P], F32, tag="zq0")
-        for i, (t, k) in enumerate(((2, 2), (3, 0), (3, 1), (3, 2))):
-            lookup((2,), t, k, room2[:, i, :])
-        part = room2[:, 13:15, :]
-        zq2 = part.rearrange("p t s -> p (t s)")
-        turn_back((2,), zq2)
-        for k in range(3):
-            lookup((3,), 1, k, room2[:, 4 + k, :])
-        zq3 = tile("zq3", [P, 4 * P], BF16)
+        terms_a = tile("terms_a", [P, PLANES * KNOTS * HALF], F32)
+        first_slopes = tile("first_slopes", [P, HALF], F32)
+        nc.vector.tensor_copy(first_slopes[:], table[0, 0][:].indirect(entries(fn_sb, 0, HALF)))
+        nc.vector.tensor_tensor(terms_a[:, :HALF], first_slopes[:], hinge[0, 0, 0], MULT)
+        add_up((0, 1), 0, 0, terms_a[:, :HALF])
+        look_up_and_add([((0, 1), t, k) for t in range(PLANES) for k in range(KNOTS)][1:], terms_a[:, HALF:])
+        z01 = tile("z01", [P, 2 * HALF], F32)
+        turn_back((0, 1), z01[:])
+
+        ahead = [((2, LAST), 0, k) for k in range(KNOTS)]
+        ahead = ahead + [((2,), t, k) for t in range(1, PLANES) for k in range(KNOTS)]
+        terms_b = tile("terms_b", [P, P * sum(len(step[0]) for step in ahead[:EARLY])], F32, reuses="hinge0_2_2")
+        look_up_and_add(ahead[:EARLY], terms_b[:])
+        deal_scales(dealt_scales[1], w2_scales_sb)
+        rounded01, accs01 = second_layer((0, 1), z01[:].bitcast(BF16))
+
+        rest = len(ahead) - EARLY
+        terms_c = tile("terms_c", [P, rest + 3 * KNOTS + 2, P], F32, reuses="z01")
+        plane1 = terms_c[:, rest : rest + KNOTS, :]
+        upper = terms_c[:, rest + KNOTS : rest + 3 * KNOTS, :]
+        partial = terms_c[:, rest + 3 * KNOTS :, :]
+        look_up_and_add(ahead[EARLY:], terms_c[:, :rest, :].rearrange("p i s -> p (i s)"))
+        z2 = partial.rearrange("p t s -> p (t s)")
+        turn_back((2,), z2)
+        look_up_and_add([((LAST,), 1, k) for k in range(KNOTS)], plane1.rearrange("p i s -> p (i s)"))
+        z3 = tile("z3", [P, PLANES * P], BF16)
         back = bank("back", [P, P])
-        nc.tensor.transpose(back[:], pairs[0, 3][:].bitcast(F32), ident[:])
-        nc.scalar.copy(zq3[:].bitcast(F32).rearrange("p (s u) -> p s u", u=2)[:, :, 0], back[:])
-        store((0, 1), accs0)
-        late = room2[:, 7:13, :]
+        nc.tensor.transpose(back[:], pairs[0, LAST][:].bitcast(F32), ident[:])
+        nc.scalar.copy(z3[:].bitcast(F32).rearrange("p (s u) -> p s u", u=2)[:, :, 0], back[:])
+        store_result((0, 1), accs01)
         for k in range(2):
-            for t in (2, 3):
-                lookup((3,), t, k, late[:, 2 * k + t - 2, :])
-        lookup((3,), 2, 2, late[:, 4, :])
-        oq2, accs2 = second((2,), zq2.bitcast(BF16), False)
-        store((2,), accs2)
-        nc.vector.tensor_tensor(part, late[:, 0:2, :], late[:, 2:4, :], ADD)
-        lookup((3,), 3, 2, late[:, 5, :])
+            for e in range(2):
+                look_up((LAST,), 2 + e, k, upper[:, 2 * k + e, :])
+        look_up((LAST,), 2, 2, upper[:, 4, :])
+        rounded2, accs2 = second_layer((2,), z2.bitcast(BF16))
+        store_result((2,), accs2)
+        nc.vector.tensor_tensor(partial, upper[:, 0:2, :], upper[:, 2:4, :], ADD)
+        look_up((LAST,), 3, 2, upper[:, 5, :])
         nc.vector.tensor_tensor(
-            zq3[:].rearrange("p (s t) -> p s t", t=4)[:, :, 2:4],
-            part.rearrange("p t s -> p s t"),
-            late[:, 4:6, :].rearrange("p t s -> p s t"),
+            z3[:].rearrange("p (s t) -> p s t", t=PLANES)[:, :, 2:4],
+            partial.rearrange("p t s -> p s t"),
+            upper[:, 4:6, :].rearrange("p t s -> p s t"),
             ADD,
         )
-        oq3 = second((3,), zq3[:], True)
-        hand_on((3,), oq3)
-        hand_on((0, 1), oq0)
-        hand_on((2,), oq2)
+
+        codes3, scales3 = quantise_z((LAST,), z3[:])
+        rounded3 = tile("rounded3", [P, PLANES * P], BF16)
+        for u, round_out in enumerate((nc.scalar.copy, nc.vector.tensor_copy)):
+            pair = slice(2 * u, 2 * u + 2)
+            acc = bank("acc", [P, 2, P])
+            for e in range(2):
+                product(1, acc[:, e, :], 2 * u + e, codes3[:], scales3[:])
+            round_out(rounded3[:].rearrange("p (s t) -> p s t", t=PLANES)[:, :, pair], acc[:].rearrange("p t s -> p s t"))
+            result = tile("result3_%d" % u, [P, 2, P], F32)
+            nc.scalar.copy(result[:], acc[:])
+            nc.sync.dma_start(out=out_rows[:, pair, columns((LAST,))], in_=result[:])
+
+        hand_on((LAST,), rounded3)
+        hand_on((0, 1), rounded01)
+        hand_on((2,), rounded2)
         for q, queue in enumerate((nc.sync, nc.scalar, nc.sync, nc.scalar)):
-            queue.dma_start(out=out_2[0, 4 * q : 4 * q + 4, :].bitcast(I32), in_=out_scales[32 * q : 32 * q + 4, :].bitcast(I32))
+            queue.dma_start(
+                out=out_2[0, 4 * q : 4 * q + 4, :].bitcast(I32), in_=out_scales[32 * q : 32 * q + 4, :].bitcast(I32)
+            )

from contextlib import ExitStack

import concourse.mybir as mybir
from concourse.masks import make_identity

F32 = mybir.dt.float32
BF16 = mybir.dt.bfloat16
I32 = mybir.dt.int32
U32 = mybir.dt.uint32
U16 = mybir.dt.uint16
U8 = mybir.dt.uint8
FP8X4 = mybir.dt.float8_e4m3fn_x4
FP4X4 = mybir.dt.float4_e2m1fn_x4
RELU = mybir.ActivationFunctionType.Relu
MULT = mybir.AluOpType.mult
ADD = mybir.AluOpType.add

P = 128
TOKENS = 2048
PICKED = 512
WIDTH = 512
HALF = 256
PLANES = 4
KNOTS = 3
KNOT = 0.75
GROUP = 16
PSUM_BANKS = 8
LAST = 3
EARLY = 8
FLOPS = 2 * 2 * WIDTH * WIDTH * PICKED


def tile_picked_kan8_none_po_kernel(
    tc, x_words, x_scales, w1_words, w1_scales, cf1, cf2, cf3, w2_words, w2_scales, offs, fn, out_0, out_1, out_2
):
    nc = tc.nc
    with ExitStack() as ctx:
        sbuf = ctx.enter_context(tc.tile_pool(name="sbuf", bufs=1))
        psum = ctx.enter_context(tc.psum_pool(name="psum", bufs=PSUM_BANKS))

        def tile(name, shape, dtype, reuses=""):
            return sbuf.tile(shape, dtype, name=name, tag=reuses or name, align_bytes=64)

        def bank(name, shape):
            return psum.tile(shape, F32, name=name, tag="bank")

        def load_scale_rows(dst, scales):
            for q in range(4):
                nc.sync.dma_start(
                    out=dst[32 * q : 32 * q + 4, :].bitcast(I32), in_=scales[0, 4 * q : 4 * q + 4, :].bitcast(I32)
                )

        def deal_words(engine, dst, src):
            engine.tensor_copy(
                out=dst[:].rearrange("p (t m b) -> p t m b", t=PLANES, b=2),
                in_=src[:].rearrange("p (m t b) -> p t m b", t=PLANES, b=2),
            )

        def deal_scales(dst, src):
            nc.vector.tensor_copy(
                out=dst[:].rearrange("p (t m) -> p t m", t=PLANES),
                in_=src[:].rearrange("p (m t) -> p t m", t=PLANES),
            )

        def entries(list_tile, first, count):
            return list_tile[:, first // GROUP : (first + count) // GROUP]

        offs_sb = tile("offs_sb", [P, PICKED // GROUP], U16)
        fn_sb = tile("fn_sb", [P, PICKED // GROUP], U16)
        x_words_sb = tile("x_words_sb", [P, TOKENS], I32)
        x_scales_sb = tile("x_scales_sb", [P, TOKENS], U8)
        w1_scales_sb = tile("w1_scales_sb", [P, WIDTH], U8)
        dealt_words = [tile("dealt_words%d" % layer, [P, 2 * WIDTH], U8) for layer in range(2)]
        dealt_scales = [tile("dealt_scales%d" % layer, [P, WIDTH], U8) for layer in range(2)]
        ident = tile("ident", [P, P], F32)
        knot_column = tile("knot_column", [P, 1], F32)
        w1_words_sb = tile("w1_words_sb", [P, 2 * WIDTH], U8)
        w2_words_sb = tile("w2_words_sb", [P, 2 * WIDTH], U8)
        w2_scales_sb = tile("w2_scales_sb", [P, WIDTH], U8)

        nc.vector.memset(x_scales_sb[:].bitcast(I32), 0)
        nc.gpsimd.memset(w1_scales_sb[:].bitcast(I32), 0)
        nc.gpsimd.memset(w2_scales_sb[:].bitcast(I32), 0)
        make_identity(nc, ident[:])
        nc.scalar.activation(knot_column[:], ident[:, 0:1], RELU, bias=KNOT, scale=0.0)
        knot_bias = (knot_column[:], 0.0, -KNOT)

        nc.sync.dma_start(offs_sb[:], offs)
        nc.sync.dma_start(out=w1_words_sb[:].bitcast(I32), in_=w1_words[0].bitcast(I32))
        nc.sync.dma_start(out=w2_words_sb[:].bitcast(I32), in_=w2_words[0].bitcast(I32))
        load_scale_rows(x_scales_sb, x_scales)
        nc.sync.dma_start(out=x_words_sb[:], in_=x_words[0].rearrange("p n t -> p (n t)").bitcast(I32))
        load_scale_rows(w1_scales_sb, w1_scales)
        nc.sync.dma_start(fn_sb[:], fn)
        table = {}
        for t in range(PLANES):
            for k, cf in enumerate((cf1, cf2, cf3)):
                table[t, k] = tile("table%d_%d" % (t, k), [P, WIDTH], F32)
                nc.sync.dma_start(out=table[t, k][:], in_=cf.rearrange("(p t) c -> p t c", t=PLANES)[:, t, :])
        load_scale_rows(w2_scales_sb, w2_scales)

        def product(layer, acc, t, codes, scales):
            nc.tensor.matmul_mx(
                out=acc,
                lhsT=dealt_words[layer][:, 2 * P * t : 2 * P * (t + 1)].bitcast(FP4X4),
                lhsT_scale=dealt_scales[layer][:, P * t : P * (t + 1)],
                rhs=codes.bitcast(FP8X4),
                rhs_scale=scales,
                start=True,
                stop=True,
            )

        deal_words(nc.vector, dealt_words[0], w1_words_sb)
        deal_words(nc.gpsimd, dealt_words[1], w2_words_sb)
        picked_scales = [tile("picked_scales%d" % half, [P, HALF], U8) for half in range(2)]
        for half in range(2):
            nc.vector.tensor_copy(picked_scales[half][:], x_scales_sb[:].indirect(entries(offs_sb, half * HALF, HALF)))
        token_words = x_words_sb[:].bitcast(U32)
        picked_words = [tile("picked_words0", [P, HALF], U32)]
        nc.vector.tensor_copy(picked_words[0][:], token_words.indirect(entries(offs_sb, 0, HALF)))
        deal_scales(dealt_scales[0], w1_scales_sb)
        picked_words.append(tile("picked_words1", [P, HALF], U32, reuses="w1_scales_sb"))
        nc.vector.tensor_copy(picked_words[1][:], token_words.indirect(entries(offs_sb, HALF, HALF)))

        hinge = {}
        banked_planes = (((0,), (1,), (2, 3)), ((0, 1), (2, 3)))
        for half in range(2):
            for planes in banked_planes[half]:
                y = bank("y", [P, len(planes), HALF])
                for i, t in enumerate(planes):
                    product(0, y[:, i, :], t, picked_words[half][:], picked_scales[half][:])
                for k in range(KNOTS):
                    relu = tile("hinge%d_%d_%d" % (half, planes[0], k), [P, len(planes), HALF], F32)
                    nc.scalar.activation(relu[:], y[:], RELU, bias=knot_bias[k])
                    for i, t in enumerate(planes):
                        hinge[half, t, k] = relu[:, i, :]

        out_scales = tile("out_scales", [P, PICKED], U8)
        out_rows = out_0.rearrange("(p t) s -> p t s", t=PLANES)
        out_words = out_1[0].rearrange("p s t -> p (s t)").bitcast(I32)
        sums = {}
        pairs = {}

        def columns(blocks):
            return slice(blocks[0] * P, (blocks[-1] + 1) * P)

        def look_up(blocks, t, k, term):
            half, first = divmod(blocks[0] * P, HALF)
            count = len(blocks) * P
            slopes = table[t, k][:].indirect(entries(fn_sb, blocks[0] * P, count))
            nc.vector.tensor_tensor(term, slopes, hinge[half, t, k][:, first : first + count], MULT)

        def add_up(blocks, t, k, term):
            u, e = divmod(t, 2)
            for i, b in enumerate(blocks):
                if e == 0 and k == 0:
                    sums[u, b] = bank("sums", [P, 2, P])
                nc.tensor.matmul(
                    sums[u, b][:, e, :],
                    lhsT=term[:, i * P : (i + 1) * P],
                    rhs=ident[:],
                    is_transpose=True,
                    start=(k == 0),
                    stop=(k == KNOTS - 1),
                )
                if e == 1 and k == KNOTS - 1:
                    pairs[u, b] = tile("pairs%d_%d" % (u, b), [P, 2 * P], BF16)
                    nc.scalar.copy(
                        pairs[u, b][:].rearrange("s (p e) -> s p e", e=2), sums[u, b][:].rearrange("s e p -> s p e")
                    )

        def look_up_and_add(steps, terms):
            first = 0
            for blocks, t, k in steps:
                term = terms[:, first : first + P * len(blocks)]
                look_up(blocks, t, k, term)
                add_up(blocks, t, k, term)
                first = first + P * len(blocks)

        def turn_back(blocks, words):
            back = bank("back", [P, len(blocks), 2, P])
            for u in range(2):
                for i, b in enumerate(blocks):
                    nc.tensor.transpose(back[:, i, u, :], pairs[u, b][:].bitcast(F32), ident[:])
            nc.scalar.copy(
                words.rearrange("p (b s u) -> p b s u", u=2, s=P), back[:].rearrange("p b u s -> p b s u")
            )

        def quantise_z(blocks, z):
            codes = tile("z_codes%d" % blocks[0], [P, len(blocks) * P], U32)
            scales = tile("z_scales%d" % blocks[0], [P, len(blocks) * P], U8)
            nc.vector.quantize_mx(out=codes[:].bitcast(FP8X4), scales=scales[:], in_=z)
            return codes, scales

        def second_layer(blocks, z):
            codes, scales = quantise_z(blocks, z)
            rounded = tile("rounded%d" % blocks[0], [P, PLANES * P * len(blocks)], BF16)
            accs = [bank("acc", [P, PLANES, P]) for b in blocks]
            for i, acc in enumerate(accs):
                for t in range(PLANES):
                    product(1, acc[:, t, :], t, codes[:, i * P : (i + 1) * P], scales[:, i * P : (i + 1) * P])
                nc.scalar.copy(
                    rounded[:, PLANES * P * i : PLANES * P * (i + 1)].rearrange("p (s t) -> p s t", t=PLANES),
                    acc[:].rearrange("p t s -> p s t"),
                )
            return rounded, accs

        def store_result(blocks, accs):
            result = tile("result%d" % blocks[0], [P, PLANES, len(blocks) * P], F32)
            for i, acc in enumerate(accs):
                nc.scalar.copy(result[:, :, i * P : (i + 1) * P], acc[:])
            nc.sync.dma_start(out=out_rows[:, :, columns(blocks)], in_=result[:])

        def hand_on(blocks, rounded):
            codes = tile("out_codes%d" % blocks[0], [P, len(blocks) * P], I32)
            nc.vector.quantize_mx(out=codes[:].bitcast(FP8X4), scales=out_scales[:, columns(blocks)], in_=rounded[:])
            nc.sync.dma_start(out=out_words[:, columns(blocks)], in_=codes[:])

        terms_a = tile("terms_a", [P, PLANES * KNOTS * HALF], F32)
        first_slopes = tile("first_slopes", [P, HALF], F32)
        nc.vector.tensor_copy(first_slopes[:], table[0, 0][:].indirect(entries(fn_sb, 0, HALF)))
        nc.vector.tensor_tensor(terms_a[:, :HALF], first_slopes[:], hinge[0, 0, 0], MULT)
        add_up((0, 1), 0, 0, terms_a[:, :HALF])
        look_up_and_add([((0, 1), t, k) for t in range(PLANES) for k in range(KNOTS)][1:], terms_a[:, HALF:])
        z01 = tile("z01", [P, 2 * HALF], F32)
        turn_back((0, 1), z01[:])

        ahead = [((2, LAST), 0, k) for k in range(KNOTS)]
        ahead = ahead + [((2,), t, k) for t in range(1, PLANES) for k in range(KNOTS)]
        terms_b = tile("terms_b", [P, P * sum(len(step[0]) for step in ahead[:EARLY])], F32, reuses="hinge0_2_2")
        look_up_and_add(ahead[:EARLY], terms_b[:])
        deal_scales(dealt_scales[1], w2_scales_sb)
        rounded01, accs01 = second_layer((0, 1), z01[:].bitcast(BF16))

        rest = len(ahead) - EARLY
        terms_c = tile("terms_c", [P, rest + 3 * KNOTS + 2, P], F32, reuses="z01")
        plane1 = terms_c[:, rest : rest + KNOTS, :]
        upper = terms_c[:, rest + KNOTS : rest + 3 * KNOTS, :]
        partial = terms_c[:, rest + 3 * KNOTS :, :]
        look_up_and_add(ahead[EARLY:], terms_c[:, :rest, :].rearrange("p i s -> p (i s)"))
        z2 = partial.rearrange("p t s -> p (t s)")
        turn_back((2,), z2)
        look_up_and_add([((LAST,), 1, k) for k in range(KNOTS)], plane1.rearrange("p i s -> p (i s)"))
        z3 = tile("z3", [P, PLANES * P], BF16)
        back = bank("back", [P, P])
        nc.tensor.transpose(back[:], pairs[0, LAST][:].bitcast(F32), ident[:])
        nc.scalar.copy(z3[:].bitcast(F32).rearrange("p (s u) -> p s u", u=2)[:, :, 0], back[:])
        store_result((0, 1), accs01)
        for k in range(2):
            for e in range(2):
                look_up((LAST,), 2 + e, k, upper[:, 2 * k + e, :])
        look_up((LAST,), 2, 2, upper[:, 4, :])
        rounded2, accs2 = second_layer((2,), z2.bitcast(BF16))
        store_result((2,), accs2)
        nc.vector.tensor_tensor(partial, upper[:, 0:2, :], upper[:, 2:4, :], ADD)
        look_up((LAST,), 3, 2, upper[:, 5, :])
        nc.vector.tensor_tensor(
            z3[:].rearrange("p (s t) -> p s t", t=PLANES)[:, :, 2:4],
            partial.rearrange("p t s -> p s t"),
            upper[:, 4:6, :].rearrange("p t s -> p s t"),
            ADD,
        )

        codes3, scales3 = quantise_z((LAST,), z3[:])
        rounded3 = tile("rounded3", [P, PLANES * P], BF16)
        for u, round_out in enumerate((nc.scalar.copy, nc.vector.tensor_copy)):
            pair = slice(2 * u, 2 * u + 2)
            acc = bank("acc", [P, 2, P])
            for e in range(2):
                product(1, acc[:, e, :], 2 * u + e, codes3[:], scales3[:])
            round_out(rounded3[:].rearrange("p (s t) -> p s t", t=PLANES)[:, :, pair], acc[:].rearrange("p t s -> p s t"))
            result = tile("result3_%d" % u, [P, 2, P], F32)
            nc.scalar.copy(result[:], acc[:])
            nc.sync.dma_start(out=out_rows[:, pair, columns((LAST,))], in_=result[:])

        hand_on((LAST,), rounded3)
        hand_on((0, 1), rounded01)
        hand_on((2,), rounded2)
        for q, queue in enumerate((nc.sync, nc.scalar, nc.sync, nc.scalar)):
            queue.dma_start(
                out=out_2[0, 4 * q : 4 * q + 4, :].bitcast(I32), in_=out_scales[32 * q : 32 * q + 4, :].bitcast(I32)
            )
